import numpy as np
import ml_dtypes


def mxq(x, axis, fmt="e4m3"):
    dtype, down = {"e4m3": (ml_dtypes.float8_e4m3fn, 7), "e5m2": (ml_dtypes.float8_e5m2, 14)}[fmt]
    v = np.moveaxis(np.asarray(x, np.float32).astype(ml_dtypes.bfloat16).astype(np.float64), axis, -1)
    blocks = v.reshape(v.shape[:-1] + (-1, 32))
    amax = np.abs(blocks).max(-1, keepdims=True)
    byte = np.maximum(np.where(amax > 0, np.frexp(amax)[1] - 1 + 127, 0) - down, 1)
    scale = np.exp2(byte - 127.0)
    codes = (blocks / scale).astype(np.float32).astype(dtype).astype(np.float64)
    return np.moveaxis((codes * scale).reshape(v.shape), -1, axis)


WIDE = False


def mx_kscale(k):
    if not WIDE:
        return np.ones(k)
    levels = np.array([10, -10, 5, -5, 0])
    if k % 512:
        return np.exp2(np.random.permutation(np.resize(levels, k // 32))).repeat(32)
    a = np.empty((k // 512, 16))
    for p in range(k // 512):
        a[p, :8] = np.random.permutation(np.resize(levels, 8))
        for g in range(8):
            far = levels[np.abs(levels - a[p, g]) >= 10]
            a[p, g + 8] = far[np.random.randint(len(far))]
    return np.exp2(a.ravel()).repeat(32)


def f64(x):
    return np.asarray(x).astype(np.float64)


def striped(idx):
    return np.tile(np.asarray(idx).reshape(-1, 16).T, (8, 1)).astype(np.uint16)


def unstriped(offs):
    return offs[:16].T.reshape(-1).astype(np.int64)


E2M1 = np.array([0.0, 0.5, 1.0, 1.5, 2.0, 3.0, 4.0, 6.0, -0.0, -0.5, -1.0, -1.5, -2.0, -3.0, -4.0, -6.0])


def pack_weight(w, fmt):
    k, n = w.shape
    w = f64(np.asarray(w, np.float32).astype(ml_dtypes.bfloat16)).reshape(k // 32, 32, n)
    amax = np.abs(w).max(1)
    if fmt == "e4m3":
        byte = np.frexp(amax)[1] - 1 + 127 - 7
    else:
        mant, ex = np.frexp(amax / 6.0)
        byte = np.where(mant > 0.5, ex, ex - 1) + 127
    byte = np.clip(np.where(amax > 0, byte, 1), 1, 254)
    scaled = (w * np.exp2(127.0 - byte)[:, None, :]).reshape(k, n).astype(np.float32)
    by_word = np.ascontiguousarray(scaled.reshape(k // 512, 128, 4, n).transpose(0, 1, 3, 2))
    if fmt == "e4m3":
        words = by_word.astype(ml_dtypes.float8_e4m3fn).view(np.uint8)
    else:
        c = by_word.astype(ml_dtypes.float4_e2m1fn).view(np.uint8) & 0xF
        words = (c[..., 0::2] | (c[..., 1::2] << 4)).reshape(k // 512, 128, 2 * n)
    return np.ascontiguousarray(words), np.ascontiguousarray(byte.astype(np.uint8).reshape(k // 512, 16, n))


def unpack_weight(words, scales, fmt):
    g, _, n = scales.shape
    words = np.ascontiguousarray(words).reshape(g, 128, n, -1)
    if fmt == "e4m3":
        vals = words.view(ml_dtypes.float8_e4m3fn).astype(np.float64)
    else:
        nib = np.empty((g, 128, n, 4), np.uint8)
        nib[..., 0::2] = words & 0xF
        nib[..., 1::2] = words >> 4
        vals = E2M1[nib]
    vals = vals * np.repeat(np.exp2(scales.astype(np.float64) - 127.0), 8, axis=1)[..., None]
    return vals.transpose(0, 1, 3, 2).reshape(g * 512, n)


D, T, I, Q, E, V, G = 512, 2048, 512, 128, 512, 16, 64


def setup_inputs():
    n = np.random.standard_normal
    idx = np.random.permutation(T)[:I]
    idx2 = np.random.permutation(T)[:I]
    fd = mx_kscale(D)
    fi = mx_kscale(I)
    ti = np.ones(T)
    ti[idx] = fi
    keysp = pack_weight(n((D, T)) / fd[:, None], "e4m3")
    return {
        "query": (n((D, Q)) * 0.9 / np.sqrt(D) * fd[:, None]).astype(np.float32),
        "keys_words": keysp[0],
        "keys_scales": keysp[1],
        "lam": (np.random.uniform(0.5, 1.5, (1, Q))).astype(np.float32),
        "cap": (np.random.uniform(0.01, 0.018, (Q, 1))).astype(np.float32),
        "os": (np.random.uniform(4.0, 16.0, (1, I)) * fi).astype(np.float32),
        "vals": (n((E, T)) / ti).astype(np.float32),
        "offs": striped(idx),
        "offs2": striped(idx2),
    }


def reference(query, keys_words, keys_scales, lam, cap, os, vals, offs, offs2):
    idx = unstriped(offs)
    idx2 = unstriped(offs2)
    keysu = unpack_weight(keys_words, keys_scales, "e4m3")
    keysidxg = keysu[:, idx]
    queryq = mxq(f64(query), 0, "e4m3")
    a0 = keysidxg.T @ queryq
    keysidx2g = keysu[:, idx2]
    b0 = keysidx2g.T @ queryq
    vo = np.tanh(a0 - b0)
    vg = vo.reshape(I, V, Q // V).mean(axis=2)
    vr = np.repeat(vg, Q // V, axis=1)
    s0 = a0 + vr * f64(lam)
    s = s0.T
    p = np.exp(s - np.max(s, axis=1, keepdims=True))
    r = p / np.sum(p, axis=1, keepdims=True)
    pg = r.reshape(Q, G, I // G).sum(axis=2)
    k0 = np.minimum(pg, f64(cap)) / pg
    kr = np.repeat(k0, I // G, axis=1)
    w = r * kr
    wo1 = w * f64(os)
    wt1 = wo1.T
    vt1 = f64(vals)[:, idx].T
    wt1q = mxq(wt1, 0, "e4m3")
    vt1q = mxq(vt1, 0, "e4m3")
    o = wt1q.T @ vt1q
    return o

@@ -1,0 +1,235 @@
+from contextlib import ExitStack
+
+import concourse.mybir as mybir
+from concourse.masks import make_identity
+
+D, T, I, Q, E = 512, 2048, 512, 128, 512
+P = 128
+PACK = 4
+GROUP = 8
+RUN = 8
+FLOPS = 2 * D * I * Q * 2 + 2 * I * Q * E
+
+F32 = mybir.dt.float32
+BF16 = mybir.dt.bfloat16
+I32 = mybir.dt.int32
+U32 = mybir.dt.uint32
+U16 = mybir.dt.uint16
+U8 = mybir.dt.uint8
+FP8X4 = mybir.dt.float8_e4m3fn_x4
+ALU = mybir.AluOpType
+ACT = mybir.ActivationFunctionType
+AXIS = mybir.AxisListType
+
+
+def tile_attend_groupvotes_runcap_read_kernel(tc, query, keys_words, keys_scales, lam, cap, slot_factor, vals, offs, offs2, out):
+    nc = tc.nc
+    half = I // 2
+    with ExitStack() as ctx:
+        sb = ctx.enter_context(tc.tile_pool(name="sb", bufs=1))
+        ps = ctx.enter_context(tc.psum_pool(name="ps", bufs=1))
+
+        key_bytes = sb.tile([P, T], U8, align_bytes=64)
+        nc.vector.memset(key_bytes[:].bitcast(I32), 0)
+        key_words = sb.tile([P, T], U32, align_bytes=64)
+        words_hbm = keys_words[0].rearrange("p t r -> p (t r)").bitcast(I32)
+        list_a = sb.tile([P, I // 16], U16)
+        nc.sync.dma_start(list_a[:], offs)
+        nc.sync.dma_start(out=key_words[:, : T // 2].bitcast(I32), in_=words_hbm[:, : T // 2])
+        list_b = sb.tile([P, I // 16], U16)
+        nc.sync.dma_start(list_b[:], offs2)
+        lam_col = sb.tile([P, 1], F32)
+        nc.sync.dma_start(out=lam_col[:], in_=lam.rearrange("o q -> q o"))
+        cap_col = sb.tile([P, 1], F32)
+        nc.sync.dma_start(out=cap_col[:], in_=cap)
+        nc.sync.dma_start(out=key_words[:, T // 2 :].bitcast(I32), in_=words_hbm[:, T // 2 :])
+        q_raw = sb.tile([P, PACK, Q], F32)
+        nc.sync.dma_start(out=q_raw[:], in_=query.rearrange("(p j) q -> p j q", j=PACK))
+        os_cols = sb.tile([P, PACK], F32)
+        nc.sync.dma_start(out=os_cols[:], in_=slot_factor.rearrange("o (p r) -> p (o r)", r=PACK))
+        scale_rows = keys_scales[0].bitcast(I32)
+        for quad in range(4):
+            nc.sync.dma_start(out=key_bytes[32 * quad : 32 * quad + 4, :].bitcast(I32), in_=scale_rows[4 * quad : 4 * quad + 4, :])
+        val_rows = []
+        for j in range(E // P):
+            rows = sb.tile([P, T], F32, tag="rows%d" % j, align_bytes=64, name="val_rows%d" % j)
+            nc.sync.dma_start(out=rows[:], in_=vals[P * j : P * (j + 1), :])
+            val_rows.append(rows)
+
+        ident = sb.tile([P, P], F32)
+        make_identity(nc, ident[:])
+
+        q_woven = sb.tile([P, Q, PACK], BF16, align_bytes=64)
+        nc.scalar.copy(out=q_woven[:], in_=q_raw[:].rearrange("p j q -> p q j"))
+        q_codes = sb.tile([P, Q], U32, align_bytes=64)
+        q_scales = sb.tile([P, Q], U8, align_bytes=64)
+        nc.vector.quantize_mx(out=q_codes[:].bitcast(FP8X4), scales=q_scales[:], in_=q_woven[:].rearrange("p q j -> p (q j)"))
+
+        a_words = sb.tile([P, I], U32, align_bytes=64)
+        b_words = sb.tile([P, I], U32, align_bytes=64)
+        nc.vector.tensor_copy(a_words[:], key_words[:].indirect(list_a[:]))
+        nc.vector.tensor_copy(b_words[:], key_words[:].indirect(list_b[:]))
+        a_scales, b_scales = [], []
+        for h in range(2):
+            for planes, offsets, name in ((a_scales, list_a, "a"), (b_scales, list_b, "b")):
+                plane = sb.tile([P, half], U8, align_bytes=64, name="%s_scales%d" % (name, h))
+                nc.vector.tensor_copy(plane[:], key_bytes[:].indirect(offsets[:, 16 * h : 16 * (h + 1)]))
+                planes.append(plane)
+
+        lam_ps = ps.tile([P, Q], F32, tag="bank6")
+        nc.tensor.transpose(lam_ps[:], lam_col[:].to_broadcast([P, P]), ident[:])
+        lam_row = sb.tile([P, Q], F32)
+        nc.scalar.activation(out=lam_row[:], in_=lam_ps[:], func=ACT.Copy, scale=1.0 / GROUP)
+
+        def scores(words, plane, h, bank):
+            tile = ps.tile([P, 2, Q], F32, tag=bank, name="scores")
+            for c in range(2):
+                nc.tensor.matmul_mx(
+                    out=tile[:, c, :],
+                    lhsT=words[:, half * h + P * c : half * h + P * (c + 1)].bitcast(FP8X4),
+                    lhsT_scale=plane[:, P * c : P * (c + 1)],
+                    rhs=q_codes[:].bitcast(FP8X4),
+                    rhs_scale=q_scales[:],
+                    start=True,
+                    stop=True,
+                )
+            return tile
+
+        a_sb, b_ps, s_ps = [], [], []
+        for h in range(2):
+            a_ps = scores(a_words, a_scales[h], h, "bank%d" % h)
+            a_sb.append(sb.tile([P, 2, Q], F32, name="a_sb%d" % h))
+            nc.scalar.copy(out=a_sb[h][:], in_=a_ps[:])
+            b_ps.append(scores(b_words, b_scales[h], h, "bank%d" % (2 + h)))
+        for h in range(2):
+            s_ps.append(ps.tile([P, half], F32, tag="bank%d" % (4 + h), name="s_ps"))
+            for c in range(2):
+                nc.tensor.matmul(s_ps[h][:, P * c : P * (c + 1)], lhsT=a_sb[h][:, c, :], rhs=ident[:], is_transpose=True, start=(c == 0), stop=False)
+
+        def pick_values(j):
+            picked = sb.tile([P, I], BF16, name="picked%d" % j)
+            nc.scalar.activation(out=picked[:], in_=val_rows[j][:].indirect(list_a[:]), func=ACT.Copy)
+            return picked
+
+        def turn_values(picked, bank, woven, copy):
+            pairs = picked[:].bitcast(F32)
+            vt_ps = ps.tile([P, 2, P], F32, tag=bank, name="vt_ps")
+            for u in range(2):
+                nc.tensor.transpose(vt_ps[:, u, :], pairs[:, u::2], ident[:])
+            copy(woven.bitcast(F32).rearrange("s (e u) -> s e u", u=2), vt_ps[:].rearrange("s u e -> s e u"))
+
+        def quantise_values(woven, tag):
+            width = woven.shape[1] // PACK
+            codes = sb.tile([P, width], U32, align_bytes=64, tag=tag, name="v_codes")
+            scales = sb.tile([P, width], U8, align_bytes=64, name="v_scales_" + tag)
+            nc.vector.quantize_mx(out=codes[:].bitcast(FP8X4), scales=scales[:], in_=woven)
+            return codes, scales
+
+        def read_out(o_ps, codes, scales):
+            nc.tensor.matmul_mx(
+                out=o_ps,
+                lhsT=w_codes[:].bitcast(FP8X4),
+                lhsT_scale=w_scales[:],
+                rhs=codes[:].bitcast(FP8X4),
+                rhs_scale=scales[:],
+                start=True,
+                stop=True,
+            )
+
+        picks = [pick_values(0)]
+        vote_tile = sb.tile([P, 4, Q], F32, tag="rows0", align_bytes=64)
+        diffs, votes, sums, lifts = [], [], [], []
+        for h in range(2):
+            diffs.append(sb.tile([P, 2, Q], F32, name="diff%d" % h))
+            votes.append(vote_tile[:, 2 * h : 2 * h + 2, :])
+            sums.append(sb.tile([P, 2, Q // GROUP], F32, name="vote_sum%d" % h))
+            lifts.append(sb.tile([P, 2, Q], F32, name="lift%d" % h))
+        for h in range(2):
+            nc.vector.tensor_tensor(diffs[h][:], a_sb[h][:], b_ps[h][:], ALU.subtract)
+            nc.scalar.activation(out=votes[h], in_=diffs[h][:], func=ACT.Tanh)
+        for h in range(2):
+            nc.vector.tensor_reduce(out=sums[h][:], in_=votes[h].rearrange("p c (v m) -> p c v m", m=GROUP), axis=AXIS.X, op=ALU.add)
+        for h in range(2):
+            nc.vector.tensor_tensor(
+                lifts[h][:].rearrange("p c (v m) -> p c v m", m=GROUP),
+                sums[h][:].unsqueeze(3).to_broadcast([P, 2, Q // GROUP, GROUP]),
+                lam_row[:].rearrange("p (v m) -> p v m", m=GROUP).unsqueeze(1).to_broadcast([P, 2, Q // GROUP, GROUP]),
+                ALU.mult,
+            )
+            for c in range(2):
+                nc.tensor.matmul(s_ps[h][:, P * c : P * (c + 1)], lhsT=lifts[h][:, c, :], rhs=ident[:], is_transpose=True, start=False, stop=(c == 1))
+
+        neg_s, neg_max = [], []
+        for h in range(2):
+            neg_s.append(sb.tile([P, half], F32, tag="neg_s%d" % h, align_bytes=64, name="neg_s%d" % h))
+            neg_max.append(sb.tile([P, 1], F32, name="neg_max%d" % h))
+            nc.vector.tensor_scalar(
+                out=neg_s[h][:],
+                in0=s_ps[h][:],
+                scalar1=-1.0,
+                scalar2=(None if h == 0 else neg_max[0][:]),
+                op0=ALU.mult,
+                op1=ALU.min,
+                accum_out=neg_max[h][:],
+            )
+        picks.append(pick_values(1))
+        p = sb.tile([P, I], F32, tag="rows1", align_bytes=64)
+        row_sums = sb.tile([P, 2], F32)
+        runs = I // RUN
+        run_sums = sb.tile([P, runs], F32)
+        run_inv = sb.tile([P, runs], F32)
+        for h in range(2):
+            nc.scalar.activation(out=p[:, half * h : half * (h + 1)], in_=neg_s[h][:], func=ACT.Exp, bias=neg_max[1][:], scale=-1.0, accum_out=row_sums[:, h : h + 1])
+        for h in range(2):
+            nc.vector.tensor_reduce(
+                out=run_sums[:, 32 * h : 32 * (h + 1)],
+                in_=p[:, half * h : half * (h + 1)].rearrange("q (g j) -> q g j", j=RUN),
+                axis=AXIS.X,
+                op=ALU.add,
+            )
+        row_sum = sb.tile([P, 1], F32)
+        nc.vector.tensor_tensor(row_sum[:], row_sums[:, 0:1], row_sums[:, 1:2], ALU.add)
+        nc.vector.reciprocal(run_inv[:, 0:32], run_sums[:, 0:32])
+        row_inv = sb.tile([P, 1], F32)
+        nc.vector.reciprocal(row_inv[:], row_sum[:])
+        nc.vector.reciprocal(run_inv[:, 32:64], run_sums[:, 32:64])
+        factor = sb.tile([P, runs], F32)
+        nc.vector.tensor_scalar(out=factor[:], in0=run_inv[:], scalar1=cap_col[:], scalar2=row_inv[:], op0=ALU.mult, op1=ALU.min)
+        w_dealt = sb.tile([P, PACK, P], F32)
+        nc.vector.tensor_tensor(
+            w_dealt[:].rearrange("q r (g e) -> q g e r", e=2),
+            p[:].rearrange("q (g e r) -> q g e r", e=2, r=PACK),
+            factor[:].unsqueeze(2).unsqueeze(3).to_broadcast([P, runs, 2, PACK]),
+            ALU.mult,
+        )
+        wt_ps = ps.tile([P, PACK, Q], F32, tag="bank0")
+        for r in range(PACK):
+            nc.tensor.transpose(wt_ps[:, r, :], w_dealt[:, r, :], ident[:])
+        w_woven = sb.tile([P, Q, PACK], BF16, align_bytes=64)
+        nc.vector.tensor_tensor(
+            w_woven[:],
+            wt_ps[:].rearrange("s r q -> s q r"),
+            os_cols[:].unsqueeze(1).to_broadcast([P, Q, PACK]),
+            ALU.mult,
+        )
+        w_codes = sb.tile([P, Q], U32, align_bytes=64)
+        w_scales = sb.tile([P, Q], U8, align_bytes=64)
+        nc.vector.quantize_mx(out=w_codes[:].bitcast(FP8X4), scales=w_scales[:], in_=w_woven[:].rearrange("s q r -> s (q r)"))
+
+        woven01 = sb.tile([P, 2 * P * PACK], BF16, align_bytes=64)
+        turn_values(picks[0], "bank3", woven01[:, : P * PACK], nc.vector.tensor_copy)
+        turn_values(picks[1], "bank4", woven01[:, P * PACK :], nc.vector.tensor_copy)
+        v01 = quantise_values(woven01[:], "neg_s1")
+        picked2 = pick_values(2)
+        picked3 = pick_values(3)
+        woven23 = sb.tile([P, 2 * P * PACK], BF16, tag="rows3", align_bytes=64)
+        turn_values(picked2, "bank1", woven23[:, : P * PACK], nc.scalar.copy)
+        turn_values(picked3, "bank2", woven23[:, P * PACK :], nc.scalar.copy)
+        v23 = quantise_values(woven23[:], "v23")
+
+        for first, v, bank, copy in ((0, v01, "bank6", nc.scalar.copy), (2, v23, "bank7", nc.vector.tensor_copy)):
+            o_ps = ps.tile([P, 2 * P], F32, tag=bank, name="o_ps")
+            read_out(o_ps[:], *v)
+            o_sb = sb.tile([P, 2 * P], F32, name="o_sb%d" % first)
+            copy(o_sb[:], o_ps[:])
+            nc.sync.dma_start(out=out[:, first * P : (first + 2) * P], in_=o_sb[:])

@@ -8,6 +8,7 @@ P = 128
 PACK = 4
 GROUP = 8
 RUN = 8
+HALF = I // 2
 FLOPS = 2 * D * I * Q * 2 + 2 * I * Q * E
 
 F32 = mybir.dt.float32
@@ -24,212 +25,221 @@ AXIS = mybir.AxisListType
 
 def tile_attend_groupvotes_runcap_read_kernel(tc, query, keys_words, keys_scales, lam, cap, slot_factor, vals, offs, offs2, out):
     nc = tc.nc
-    half = I // 2
     with ExitStack() as ctx:
         sb = ctx.enter_context(tc.tile_pool(name="sb", bufs=1))
         ps = ctx.enter_context(tc.psum_pool(name="ps", bufs=1))
 
-        key_bytes = sb.tile([P, T], U8, align_bytes=64)
+        def sbuf(name, shape, dtype, reuse=None):
+            return sb.tile(shape, dtype, name=name, tag=reuse or name, align_bytes=64)
+
+        def bank(number, shape):
+            return ps.tile(shape, F32, name="bank%d" % number, tag="bank%d" % number)
+
+        def quantise(name, woven, reuse=None):
+            width = woven.shape[1] // PACK
+            codes = sbuf(name + "_codes", [P, width], U32, reuse)
+            scales = sbuf(name + "_scales", [P, width], U8)
+            nc.vector.quantize_mx(out=codes[:].bitcast(FP8X4), scales=scales[:], in_=woven)
+            return codes, scales
+
+        def product(dst, lhs_codes, lhs_scales, rhs_codes, rhs_scales):
+            nc.tensor.matmul_mx(
+                out=dst,
+                lhsT=lhs_codes.bitcast(FP8X4),
+                lhsT_scale=lhs_scales,
+                rhs=rhs_codes.bitcast(FP8X4),
+                rhs_scale=rhs_scales,
+                start=True,
+                stop=True,
+            )
+
+        key_bytes = sbuf("key_bytes", [P, T], U8)
         nc.vector.memset(key_bytes[:].bitcast(I32), 0)
-        key_words = sb.tile([P, T], U32, align_bytes=64)
-        words_hbm = keys_words[0].rearrange("p t r -> p (t r)").bitcast(I32)
         list_a = sb.tile([P, I // 16], U16)
         nc.sync.dma_start(list_a[:], offs)
-        nc.sync.dma_start(out=key_words[:, : T // 2].bitcast(I32), in_=words_hbm[:, : T // 2])
         list_b = sb.tile([P, I // 16], U16)
         nc.sync.dma_start(list_b[:], offs2)
-        lam_col = sb.tile([P, 1], F32)
-        nc.sync.dma_start(out=lam_col[:], in_=lam.rearrange("o q -> q o"))
-        cap_col = sb.tile([P, 1], F32)
-        nc.sync.dma_start(out=cap_col[:], in_=cap)
-        nc.sync.dma_start(out=key_words[:, T // 2 :].bitcast(I32), in_=words_hbm[:, T // 2 :])
-        q_raw = sb.tile([P, PACK, Q], F32)
-        nc.sync.dma_start(out=q_raw[:], in_=query.rearrange("(p j) q -> p j q", j=PACK))
-        os_cols = sb.tile([P, PACK], F32)
-        nc.sync.dma_start(out=os_cols[:], in_=slot_factor.rearrange("o (p r) -> p (o r)", r=PACK))
+        q_raw = sbuf("q_raw", [P, PACK, Q], F32)
+        nc.scalar.dma_start(out=q_raw[:], in_=query.rearrange("(p j) q -> p j q", j=PACK))
         scale_rows = keys_scales[0].bitcast(I32)
-        for quad in range(4):
-            nc.sync.dma_start(out=key_bytes[32 * quad : 32 * quad + 4, :].bitcast(I32), in_=scale_rows[4 * quad : 4 * quad + 4, :])
-        val_rows = []
-        for j in range(E // P):
-            rows = sb.tile([P, T], F32, tag="rows%d" % j, align_bytes=64, name="val_rows%d" % j)
-            nc.sync.dma_start(out=rows[:], in_=vals[P * j : P * (j + 1), :])
-            val_rows.append(rows)
+        for quad, queue in enumerate((nc.sync, nc.sync, nc.scalar, nc.scalar)):
+            queue.dma_start(out=key_bytes[32 * quad : 32 * quad + 4, :].bitcast(I32), in_=scale_rows[4 * quad : 4 * quad + 4, :])
+        key_words = sbuf("key_words", [P, T], U32)
+        nc.sync.dma_start(out=key_words[:].bitcast(I32), in_=keys_words[0].rearrange("p t r -> p (t r)").bitcast(I32))
+        lam_col = sbuf("lam_col", [P, 1], F32)
+        nc.sync.dma_start(out=lam_col[:], in_=lam.rearrange("o q -> q o"))
 
-        ident = sb.tile([P, P], F32)
+        def load_values(j):
+            rows = sbuf("val_rows%d" % j, [P, T], F32)
+            nc.sync.dma_start(out=rows[:], in_=vals[P * j : P * (j + 1), :])
+            return rows
+
+        val_rows = [load_values(0)]
+        cap_col = sbuf("cap_col", [P, 1], F32)
+        nc.sync.dma_start(out=cap_col[:], in_=cap)
+        os_cols = sbuf("os_cols", [P, PACK], F32)
+        nc.sync.dma_start(out=os_cols[:], in_=slot_factor.rearrange("o (p r) -> p (o r)", r=PACK))
+        for j in range(1, E // P):
+            val_rows.append(load_values(j))
+
+        ident = sbuf("ident", [P, P], F32)
         make_identity(nc, ident[:])
 
-        q_woven = sb.tile([P, Q, PACK], BF16, align_bytes=64)
+        picked_bytes = []
+        for side, offsets in enumerate((list_a, list_b)):
+            picked_bytes.append(sbuf("picked_bytes%d" % side, [P, I], U8))
+            nc.vector.tensor_copy(picked_bytes[side][:], key_bytes[:].indirect(offsets[:]))
+
+        q_woven = sbuf("q_woven", [P, Q, PACK], BF16)
         nc.scalar.copy(out=q_woven[:], in_=q_raw[:].rearrange("p j q -> p q j"))
-        q_codes = sb.tile([P, Q], U32, align_bytes=64)
-        q_scales = sb.tile([P, Q], U8, align_bytes=64)
-        nc.vector.quantize_mx(out=q_codes[:].bitcast(FP8X4), scales=q_scales[:], in_=q_woven[:].rearrange("p q j -> p (q j)"))
+        q_codes, q_scales = quantise("q", q_woven[:].rearrange("p q j -> p (q j)"))
 
-        a_words = sb.tile([P, I], U32, align_bytes=64)
-        b_words = sb.tile([P, I], U32, align_bytes=64)
-        nc.vector.tensor_copy(a_words[:], key_words[:].indirect(list_a[:]))
-        nc.vector.tensor_copy(b_words[:], key_words[:].indirect(list_b[:]))
-        a_scales, b_scales = [], []
+        picked_words = {}
         for h in range(2):
-            for planes, offsets, name in ((a_scales, list_a, "a"), (b_scales, list_b, "b")):
-                plane = sb.tile([P, half], U8, align_bytes=64, name="%s_scales%d" % (name, h))
-                nc.vector.tensor_copy(plane[:], key_bytes[:].indirect(offsets[:, 16 * h : 16 * (h + 1)]))
-                planes.append(plane)
+            for side, offsets in enumerate((list_a, list_b)):
+                picked_words[side, h] = sbuf("picked_words%d%d" % (side, h), [P, HALF], U32)
+                nc.vector.tensor_copy(picked_words[side, h][:], key_words[:].indirect(offsets[:, 16 * h : 16 * (h + 1)]))
 
-        lam_ps = ps.tile([P, Q], F32, tag="bank6")
+        lam_ps = bank(6, [P, Q])
         nc.tensor.transpose(lam_ps[:], lam_col[:].to_broadcast([P, P]), ident[:])
-        lam_row = sb.tile([P, Q], F32)
+        lam_row = sbuf("lam_row", [P, Q], F32)
         nc.scalar.activation(out=lam_row[:], in_=lam_ps[:], func=ACT.Copy, scale=1.0 / GROUP)
 
-        def scores(words, plane, h, bank):
-            tile = ps.tile([P, 2, Q], F32, tag=bank, name="scores")
+        def scores(side, h):
+            tile = bank(2 * side + h, [P, 2, Q])
             for c in range(2):
-                nc.tensor.matmul_mx(
-                    out=tile[:, c, :],
-                    lhsT=words[:, half * h + P * c : half * h + P * (c + 1)].bitcast(FP8X4),
-                    lhsT_scale=plane[:, P * c : P * (c + 1)],
-                    rhs=q_codes[:].bitcast(FP8X4),
-                    rhs_scale=q_scales[:],
-                    start=True,
-                    stop=True,
+                slot = HALF * h + P * c
+                product(
+                    tile[:, c, :],
+                    picked_words[side, h][:, P * c : P * (c + 1)],
+                    picked_bytes[side][:, slot : slot + P],
+                    q_codes[:],
+                    q_scales[:],
                 )
             return tile
 
         a_sb, b_ps, s_ps = [], [], []
         for h in range(2):
-            a_ps = scores(a_words, a_scales[h], h, "bank%d" % h)
-            a_sb.append(sb.tile([P, 2, Q], F32, name="a_sb%d" % h))
+            a_ps = scores(0, h)
+            a_sb.append(sbuf("a_sb%d" % h, [P, 2, Q], F32))
             nc.scalar.copy(out=a_sb[h][:], in_=a_ps[:])
-            b_ps.append(scores(b_words, b_scales[h], h, "bank%d" % (2 + h)))
+            b_ps.append(scores(1, h))
         for h in range(2):
-            s_ps.append(ps.tile([P, half], F32, tag="bank%d" % (4 + h), name="s_ps"))
+            s_ps.append(bank(4 + h, [P, HALF]))
             for c in range(2):
                 nc.tensor.matmul(s_ps[h][:, P * c : P * (c + 1)], lhsT=a_sb[h][:, c, :], rhs=ident[:], is_transpose=True, start=(c == 0), stop=False)
 
-        def pick_values(j):
-            picked = sb.tile([P, I], BF16, name="picked%d" % j)
-            nc.scalar.activation(out=picked[:], in_=val_rows[j][:].indirect(list_a[:]), func=ACT.Copy)
-            return picked
-
-        def turn_values(picked, bank, woven, copy):
-            pairs = picked[:].bitcast(F32)
-            vt_ps = ps.tile([P, 2, P], F32, tag=bank, name="vt_ps")
-            for u in range(2):
-                nc.tensor.transpose(vt_ps[:, u, :], pairs[:, u::2], ident[:])
-            copy(woven.bitcast(F32).rearrange("s (e u) -> s e u", u=2), vt_ps[:].rearrange("s u e -> s e u"))
-
-        def quantise_values(woven, tag):
-            width = woven.shape[1] // PACK
-            codes = sb.tile([P, width], U32, align_bytes=64, tag=tag, name="v_codes")
-            scales = sb.tile([P, width], U8, align_bytes=64, name="v_scales_" + tag)
-            nc.vector.quantize_mx(out=codes[:].bitcast(FP8X4), scales=scales[:], in_=woven)
-            return codes, scales
-
-        def read_out(o_ps, codes, scales):
-            nc.tensor.matmul_mx(
-                out=o_ps,
-                lhsT=w_codes[:].bitcast(FP8X4),
-                lhsT_scale=w_scales[:],
-                rhs=codes[:].bitcast(FP8X4),
-                rhs_scale=scales[:],
-                start=True,
-                stop=True,
-            )
-
-        picks = [pick_values(0)]
-        vote_tile = sb.tile([P, 4, Q], F32, tag="rows0", align_bytes=64)
-        diffs, votes, sums, lifts = [], [], [], []
+        votes, sums = [], []
         for h in range(2):
-            diffs.append(sb.tile([P, 2, Q], F32, name="diff%d" % h))
-            votes.append(vote_tile[:, 2 * h : 2 * h + 2, :])
-            sums.append(sb.tile([P, 2, Q // GROUP], F32, name="vote_sum%d" % h))
-            lifts.append(sb.tile([P, 2, Q], F32, name="lift%d" % h))
+            diff = sbuf("diff%d" % h, [P, 2, Q], F32)
+            nc.vector.tensor_tensor(diff[:], a_sb[h][:], b_ps[h][:], ALU.subtract)
+            votes.append(sbuf("vote%d" % h, [P, 2, Q], F32))
+            nc.scalar.activation(out=votes[h][:], in_=diff[:], func=ACT.Tanh)
         for h in range(2):
-            nc.vector.tensor_tensor(diffs[h][:], a_sb[h][:], b_ps[h][:], ALU.subtract)
-            nc.scalar.activation(out=votes[h], in_=diffs[h][:], func=ACT.Tanh)
+            sums.append(sbuf("vote_sum%d" % h, [P, 2, Q // GROUP], F32))
+            nc.vector.tensor_reduce(out=sums[h][:], in_=votes[h][:].rearrange("p c (v m) -> p c v m", m=GROUP), axis=AXIS.X, op=ALU.add)
         for h in range(2):
-            nc.vector.tensor_reduce(out=sums[h][:], in_=votes[h].rearrange("p c (v m) -> p c v m", m=GROUP), axis=AXIS.X, op=ALU.add)
-        for h in range(2):
+            lift = sbuf("lift%d" % h, [P, 2, Q], F32)
             nc.vector.tensor_tensor(
-                lifts[h][:].rearrange("p c (v m) -> p c v m", m=GROUP),
+                lift[:].rearrange("p c (v m) -> p c v m", m=GROUP),
                 sums[h][:].unsqueeze(3).to_broadcast([P, 2, Q // GROUP, GROUP]),
                 lam_row[:].rearrange("p (v m) -> p v m", m=GROUP).unsqueeze(1).to_broadcast([P, 2, Q // GROUP, GROUP]),
                 ALU.mult,
             )
             for c in range(2):
-                nc.tensor.matmul(s_ps[h][:, P * c : P * (c + 1)], lhsT=lifts[h][:, c, :], rhs=ident[:], is_transpose=True, start=False, stop=(c == 1))
+                nc.tensor.matmul(s_ps[h][:, P * c : P * (c + 1)], lhsT=lift[:, c, :], rhs=ident[:], is_transpose=True, start=False, stop=(c == 1))
 
         neg_s, neg_max = [], []
         for h in range(2):
-            neg_s.append(sb.tile([P, half], F32, tag="neg_s%d" % h, align_bytes=64, name="neg_s%d" % h))
-            neg_max.append(sb.tile([P, 1], F32, name="neg_max%d" % h))
+            neg_s.append(sbuf("neg_s%d" % h, [P, PACK, P // 2], F32))
+            neg_max.append(sbuf("neg_max%d" % h, [P, 1], F32))
             nc.vector.tensor_scalar(
                 out=neg_s[h][:],
-                in0=s_ps[h][:],
+                in0=s_ps[h][:].rearrange("q (s r) -> q r s", r=PACK),
                 scalar1=-1.0,
                 scalar2=(None if h == 0 else neg_max[0][:]),
                 op0=ALU.mult,
                 op1=ALU.min,
                 accum_out=neg_max[h][:],
             )
-        picks.append(pick_values(1))
-        p = sb.tile([P, I], F32, tag="rows1", align_bytes=64)
-        row_sums = sb.tile([P, 2], F32)
+        p = sbuf("p", [P, PACK, P], F32)
+        row_sums = sbuf("row_sums", [P, 2], F32)
         runs = I // RUN
-        run_sums = sb.tile([P, runs], F32)
-        run_inv = sb.tile([P, runs], F32)
+        run_sums = sbuf("run_sums", [P, runs], F32)
+        run_inv = sbuf("run_inv", [P, runs], F32)
         for h in range(2):
-            nc.scalar.activation(out=p[:, half * h : half * (h + 1)], in_=neg_s[h][:], func=ACT.Exp, bias=neg_max[1][:], scale=-1.0, accum_out=row_sums[:, h : h + 1])
+            part = p[:, :, P // 2 * h : P // 2 * (h + 1)]
+            nc.scalar.activation(out=part, in_=neg_s[h][:], func=ACT.Exp, bias=neg_max[1][:], scale=-1.0, accum_out=row_sums[:, h : h + 1])
+        row_sum = sbuf("row_sum", [P, 1], F32)
+        row_inv = sbuf("row_inv", [P, 1], F32)
         for h in range(2):
-            nc.vector.tensor_reduce(
-                out=run_sums[:, 32 * h : 32 * (h + 1)],
-                in_=p[:, half * h : half * (h + 1)].rearrange("q (g j) -> q g j", j=RUN),
-                axis=AXIS.X,
-                op=ALU.add,
-            )
-        row_sum = sb.tile([P, 1], F32)
+            part = p[:, :, P // 2 * h : P // 2 * (h + 1)]
+            nc.vector.tensor_reduce(out=run_sums[:, runs // 2 * h : runs // 2 * (h + 1)], in_=part.rearrange("q r (g e) -> q g r e", e=2), axis=AXIS.XY, op=ALU.add)
         nc.vector.tensor_tensor(row_sum[:], row_sums[:, 0:1], row_sums[:, 1:2], ALU.add)
-        nc.vector.reciprocal(run_inv[:, 0:32], run_sums[:, 0:32])
-        row_inv = sb.tile([P, 1], F32)
+        nc.vector.reciprocal(run_inv[:, : runs // 2], run_sums[:, : runs // 2])
         nc.vector.reciprocal(row_inv[:], row_sum[:])
-        nc.vector.reciprocal(run_inv[:, 32:64], run_sums[:, 32:64])
-        factor = sb.tile([P, runs], F32)
-        nc.vector.tensor_scalar(out=factor[:], in0=run_inv[:], scalar1=cap_col[:], scalar2=row_inv[:], op0=ALU.mult, op1=ALU.min)
-        w_dealt = sb.tile([P, PACK, P], F32)
-        nc.vector.tensor_tensor(
-            w_dealt[:].rearrange("q r (g e) -> q g e r", e=2),
-            p[:].rearrange("q (g e r) -> q g e r", e=2, r=PACK),
-            factor[:].unsqueeze(2).unsqueeze(3).to_broadcast([P, runs, 2, PACK]),
-            ALU.mult,
+        nc.vector.reciprocal(run_inv[:, runs // 2 :], run_sums[:, runs // 2 :])
+        factor = sbuf("factor", [P, runs, 2], F32)
+        nc.vector.tensor_scalar(
+            out=factor[:],
+            in0=run_inv[:].unsqueeze(2).to_broadcast([P, runs, 2]),
+            scalar1=cap_col[:],
+            scalar2=row_inv[:],
+            op0=ALU.mult,
+            op1=ALU.min,
         )
-        wt_ps = ps.tile([P, PACK, Q], F32, tag="bank0")
+
+        def pick_values(j, reuse, on_vector):
+            picked = sbuf("picked%d" % j, [P, I], BF16, reuse)
+            if on_vector > 0:
+                nc.vector.tensor_copy(picked[:, :on_vector], val_rows[j][:].indirect(list_a[:, : on_vector // 16]))
+            if on_vector < I:
+                nc.scalar.activation(out=picked[:, on_vector:], in_=val_rows[j][:].indirect(list_a[:, on_vector // 16 :]), func=ACT.Copy)
+            return picked
+
+        def turn_values(picked, number, pairs_out, copy):
+            pairs = picked[:].bitcast(F32)
+            turned = bank(number, [P, 2, P])
+            for u in range(2):
+                nc.tensor.transpose(turned[:, u, :], pairs[:, u::2], ident[:])
+            copy(pairs_out.rearrange("s (e u) -> s e u", u=2), turned[:].rearrange("s u e -> s e u"))
+
+        picked = [
+            pick_values(0, "diff1", 0),
+            pick_values(1, None, HALF),
+            pick_values(2, "neg_s1", 0),
+            pick_values(3, "run_inv", I),
+        ]
+        woven01 = sbuf("woven01", [P, 4 * P], F32)
+        turn_values(picked[0], 4, woven01[:, : 2 * P], nc.vector.tensor_copy)
+        turn_values(picked[1], 5, woven01[:, 2 * P :], nc.vector.tensor_copy)
+
+        pt_ps = bank(0, [P, PACK, Q])
         for r in range(PACK):
-            nc.tensor.transpose(wt_ps[:, r, :], w_dealt[:, r, :], ident[:])
-        w_woven = sb.tile([P, Q, PACK], BF16, align_bytes=64)
+            nc.tensor.transpose(pt_ps[:, r, :], p[:, r, :], ident[:])
+        pt_os = sbuf("pt_os", [P, PACK, Q], F32, "val_rows2")
+        for r in range(PACK):
+            nc.scalar.activation(out=pt_os[:, r, :], in_=pt_ps[:, r, :], func=ACT.Copy, scale=os_cols[:, r : r + 1])
+        factor_ps = bank(1, [P, Q])
+        nc.tensor.transpose(factor_ps[:], factor[:].rearrange("q g e -> q (g e)"), ident[:])
+        w_woven = sbuf("w_woven", [P, Q, PACK], BF16, "val_rows3")
         nc.vector.tensor_tensor(
             w_woven[:],
-            wt_ps[:].rearrange("s r q -> s q r"),
-            os_cols[:].unsqueeze(1).to_broadcast([P, Q, PACK]),
+            pt_os[:].rearrange("s r q -> s q r"),
+            factor_ps[:].unsqueeze(2).to_broadcast([P, Q, PACK]),
             ALU.mult,
         )
-        w_codes = sb.tile([P, Q], U32, align_bytes=64)
-        w_scales = sb.tile([P, Q], U8, align_bytes=64)
-        nc.vector.quantize_mx(out=w_codes[:].bitcast(FP8X4), scales=w_scales[:], in_=w_woven[:].rearrange("s q r -> s (q r)"))
+        w_codes, w_scales = quantise("w", w_woven[:].rearrange("s q r -> s (q r)"))
+        v01 = quantise("v01", woven01[:].bitcast(BF16), "val_rows2")
 
-        woven01 = sb.tile([P, 2 * P * PACK], BF16, align_bytes=64)
-        turn_values(picks[0], "bank3", woven01[:, : P * PACK], nc.vector.tensor_copy)
-        turn_values(picks[1], "bank4", woven01[:, P * PACK :], nc.vector.tensor_copy)
-        v01 = quantise_values(woven01[:], "neg_s1")
-        picked2 = pick_values(2)
-        picked3 = pick_values(3)
-        woven23 = sb.tile([P, 2 * P * PACK], BF16, tag="rows3", align_bytes=64)
-        turn_values(picked2, "bank1", woven23[:, : P * PACK], nc.scalar.copy)
-        turn_values(picked3, "bank2", woven23[:, P * PACK :], nc.scalar.copy)
-        v23 = quantise_values(woven23[:], "v23")
+        woven23 = sbuf("woven23", [P, 4 * P], F32)
+        turn_values(picked[2], 3, woven23[:, : 2 * P], nc.scalar.copy)
+        turn_values(picked[3], 2, woven23[:, 2 * P :], nc.scalar.copy)
+        v23 = quantise("v23", woven23[:].bitcast(BF16))
 
-        for first, v, bank, copy in ((0, v01, "bank6", nc.scalar.copy), (2, v23, "bank7", nc.vector.tensor_copy)):
-            o_ps = ps.tile([P, 2 * P], F32, tag=bank, name="o_ps")
-            read_out(o_ps[:], *v)
-            o_sb = sb.tile([P, 2 * P], F32, name="o_sb%d" % first)
-            copy(o_sb[:], o_ps[:])
-            nc.sync.dma_start(out=out[:, first * P : (first + 2) * P], in_=o_sb[:])
+        for first, (codes, scales), copy in ((0, v01, nc.scalar.copy), (2, v23, nc.vector.tensor_copy)):
+            result_ps = bank(6 + first // 2, [P, 2 * P])
+            product(result_ps[:], w_codes[:], w_scales[:], codes[:], scales[:])
+            result = sbuf("result%d" % first, [P, 2 * P], F32)
+            copy(result[:], result_ps[:])
+            nc.sync.dma_start(out=out[:, first * P : (first + 2) * P], in_=result[:])

@@ -54,16 +54,16 @@ def tile_attend_groupvotes_runcap_read_kernel(tc, query, keys_words, keys_scales
             )
 
         key_bytes = sbuf("key_bytes", [P, T], U8)
-        nc.vector.memset(key_bytes[:].bitcast(I32), 0)
+        nc.gpsimd.memset(key_bytes[:].bitcast(I32), 0)
         list_a = sb.tile([P, I // 16], U16)
         nc.sync.dma_start(list_a[:], offs)
+        scale_rows = keys_scales[0].bitcast(I32)
+        for quad in range(4):
+            nc.sync.dma_start(out=key_bytes[32 * quad : 32 * quad + 4, :].bitcast(I32), in_=scale_rows[4 * quad : 4 * quad + 4, :])
         list_b = sb.tile([P, I // 16], U16)
         nc.sync.dma_start(list_b[:], offs2)
         q_raw = sbuf("q_raw", [P, PACK, Q], F32)
-        nc.scalar.dma_start(out=q_raw[:], in_=query.rearrange("(p j) q -> p j q", j=PACK))
-        scale_rows = keys_scales[0].bitcast(I32)
-        for quad, queue in enumerate((nc.sync, nc.sync, nc.scalar, nc.scalar)):
-            queue.dma_start(out=key_bytes[32 * quad : 32 * quad + 4, :].bitcast(I32), in_=scale_rows[4 * quad : 4 * quad + 4, :])
+        nc.sync.dma_start(out=q_raw[:], in_=query.rearrange("(p j) q -> p j q", j=PACK))
         key_words = sbuf("key_words", [P, T], U32)
         nc.sync.dma_start(out=key_words[:].bitcast(I32), in_=keys_words[0].rearrange("p t r -> p (t r)").bitcast(I32))
         lam_col = sbuf("lam_col", [P, 1], F32)
@@ -149,96 +149,93 @@ def tile_attend_groupvotes_runcap_read_kernel(tc, query, keys_words, keys_scales
             for c in range(2):
                 nc.tensor.matmul(s_ps[h][:, P * c : P * (c + 1)], lhsT=lift[:, c, :], rhs=ident[:], is_transpose=True, start=False, stop=(c == 1))
 
+        def pick_values(j):
+            picked = sbuf("picked%d" % j, [P, I], BF16)
+            nc.scalar.activation(out=picked[:], in_=val_rows[j][:].indirect(list_a[:]), func=ACT.Copy)
+            return picked
+
         neg_s, neg_max = [], []
         for h in range(2):
-            neg_s.append(sbuf("neg_s%d" % h, [P, PACK, P // 2], F32))
+            neg_s.append(sbuf("neg_s%d" % h, [P, HALF], F32))
             neg_max.append(sbuf("neg_max%d" % h, [P, 1], F32))
             nc.vector.tensor_scalar(
                 out=neg_s[h][:],
-                in0=s_ps[h][:].rearrange("q (s r) -> q r s", r=PACK),
+                in0=s_ps[h][:],
                 scalar1=-1.0,
                 scalar2=(None if h == 0 else neg_max[0][:]),
                 op0=ALU.mult,
                 op1=ALU.min,
                 accum_out=neg_max[h][:],
             )
-        p = sbuf("p", [P, PACK, P], F32)
+        half_runs = HALF // RUN
+        run_sums, run_inv, factor = [], [], []
         row_sums = sbuf("row_sums", [P, 2], F32)
-        runs = I // RUN
-        run_sums = sbuf("run_sums", [P, runs], F32)
-        run_inv = sbuf("run_inv", [P, runs], F32)
+        picked = [pick_values(0), pick_values(1)]
+        p_tile = sbuf("p", [P, I], F32, "val_rows1")
+        p = [p_tile[:, :HALF], p_tile[:, HALF:]]
         for h in range(2):
-            part = p[:, :, P // 2 * h : P // 2 * (h + 1)]
-            nc.scalar.activation(out=part, in_=neg_s[h][:], func=ACT.Exp, bias=neg_max[1][:], scale=-1.0, accum_out=row_sums[:, h : h + 1])
+            nc.scalar.activation(out=p[h], in_=neg_s[h][:], func=ACT.Exp, bias=neg_max[1][:], scale=-1.0, accum_out=row_sums[:, h : h + 1])
+        for h in range(2):
+            run_sums.append(sbuf("run_sums%d" % h, [P, half_runs], F32))
+            nc.vector.tensor_reduce(out=run_sums[h][:], in_=p[h].rearrange("q (g j) -> q g j", j=RUN), axis=AXIS.X, op=ALU.add)
         row_sum = sbuf("row_sum", [P, 1], F32)
+        nc.vector.tensor_tensor(row_sum[:], row_sums[:, 0:1], row_sums[:, 1:2], ALU.add)
         row_inv = sbuf("row_inv", [P, 1], F32)
         for h in range(2):
-            part = p[:, :, P // 2 * h : P // 2 * (h + 1)]
-            nc.vector.tensor_reduce(out=run_sums[:, runs // 2 * h : runs // 2 * (h + 1)], in_=part.rearrange("q r (g e) -> q g r e", e=2), axis=AXIS.XY, op=ALU.add)
-        nc.vector.tensor_tensor(row_sum[:], row_sums[:, 0:1], row_sums[:, 1:2], ALU.add)
-        nc.vector.reciprocal(run_inv[:, : runs // 2], run_sums[:, : runs // 2])
-        nc.vector.reciprocal(row_inv[:], row_sum[:])
-        nc.vector.reciprocal(run_inv[:, runs // 2 :], run_sums[:, runs // 2 :])
-        factor = sbuf("factor", [P, runs, 2], F32)
-        nc.vector.tensor_scalar(
-            out=factor[:],
-            in0=run_inv[:].unsqueeze(2).to_broadcast([P, runs, 2]),
-            scalar1=cap_col[:],
-            scalar2=row_inv[:],
-            op0=ALU.mult,
-            op1=ALU.min,
-        )
-
-        def pick_values(j, reuse, on_vector):
-            picked = sbuf("picked%d" % j, [P, I], BF16, reuse)
-            if on_vector > 0:
-                nc.vector.tensor_copy(picked[:, :on_vector], val_rows[j][:].indirect(list_a[:, : on_vector // 16]))
-            if on_vector < I:
-                nc.scalar.activation(out=picked[:, on_vector:], in_=val_rows[j][:].indirect(list_a[:, on_vector // 16 :]), func=ACT.Copy)
-            return picked
-
-        def turn_values(picked, number, pairs_out, copy):
-            pairs = picked[:].bitcast(F32)
-            turned = bank(number, [P, 2, P])
-            for u in range(2):
-                nc.tensor.transpose(turned[:, u, :], pairs[:, u::2], ident[:])
-            copy(pairs_out.rearrange("s (e u) -> s e u", u=2), turned[:].rearrange("s u e -> s e u"))
-
-        picked = [
-            pick_values(0, "diff1", 0),
-            pick_values(1, None, HALF),
-            pick_values(2, "neg_s1", 0),
-            pick_values(3, "run_inv", I),
-        ]
-        woven01 = sbuf("woven01", [P, 4 * P], F32)
-        turn_values(picked[0], 4, woven01[:, : 2 * P], nc.vector.tensor_copy)
-        turn_values(picked[1], 5, woven01[:, 2 * P :], nc.vector.tensor_copy)
-
-        pt_ps = bank(0, [P, PACK, Q])
+            run_inv.append(sbuf("run_inv%d" % h, [P, half_runs], F32))
+            nc.vector.reciprocal(run_inv[h][:], run_sums[h][:])
+            if h == 0:
+                nc.vector.reciprocal(row_inv[:], row_sum[:])
+        for h in range(2):
+            factor.append(sbuf("factor%d" % h, [P, half_runs, 2], F32))
+            nc.vector.tensor_scalar(
+                out=factor[h][:],
+                in0=run_inv[h][:].unsqueeze(2).to_broadcast([P, half_runs, 2]),
+                scalar1=cap_col[:],
+                scalar2=row_inv[:],
+                op0=ALU.mult,
+                op1=ALU.min,
+            )
+        w_dealt = sbuf("w_dealt", [P, PACK, P], F32)
+        for h in range(2):
+            nc.vector.tensor_tensor(
+                w_dealt[:, :, P // 2 * h : P // 2 * (h + 1)].rearrange("q r (b s) -> q b r s", s=4),
+                p[h].rearrange("q (b s r) -> q b r s", s=4, r=PACK),
+                factor[h][:].rearrange("q (b g) e -> q b (g e)", g=2).unsqueeze(2).to_broadcast([P, P // 8, PACK, 4]),
+                ALU.mult,
+            )
+        wt_ps = bank(0, [P, PACK, Q])
         for r in range(PACK):
-            nc.tensor.transpose(pt_ps[:, r, :], p[:, r, :], ident[:])
-        pt_os = sbuf("pt_os", [P, PACK, Q], F32, "val_rows2")
-        for r in range(PACK):
-            nc.scalar.activation(out=pt_os[:, r, :], in_=pt_ps[:, r, :], func=ACT.Copy, scale=os_cols[:, r : r + 1])
-        factor_ps = bank(1, [P, Q])
-        nc.tensor.transpose(factor_ps[:], factor[:].rearrange("q g e -> q (g e)"), ident[:])
-        w_woven = sbuf("w_woven", [P, Q, PACK], BF16, "val_rows3")
+            nc.tensor.transpose(wt_ps[:, r, :], w_dealt[:, r, :], ident[:])
+        w_woven = sbuf("w_woven", [P, Q, PACK], BF16)
         nc.vector.tensor_tensor(
             w_woven[:],
-            pt_os[:].rearrange("s r q -> s q r"),
-            factor_ps[:].unsqueeze(2).to_broadcast([P, Q, PACK]),
+            wt_ps[:].rearrange("s r q -> s q r"),
+            os_cols[:].unsqueeze(1).to_broadcast([P, Q, PACK]),
             ALU.mult,
         )
         w_codes, w_scales = quantise("w", w_woven[:].rearrange("s q r -> s (q r)"))
-        v01 = quantise("v01", woven01[:].bitcast(BF16), "val_rows2")
 
-        woven23 = sbuf("woven23", [P, 4 * P], F32)
-        turn_values(picked[2], 3, woven23[:, : 2 * P], nc.scalar.copy)
-        turn_values(picked[3], 2, woven23[:, 2 * P :], nc.scalar.copy)
+        def turn_values(j, number, copy):
+            pairs = picked[j][:].bitcast(F32)
+            turned = bank(number, [P, 2, P])
+            for u in range(2):
+                nc.tensor.transpose(turned[:, u, :], pairs[:, u::2], ident[:])
+            copy(woven[j].rearrange("s (e u) -> s e u", u=2), turned[:].rearrange("s u e -> s e u"))
+
+        picked.extend([pick_values(2), pick_values(3)])
+        woven01 = sbuf("woven01", [P, 4 * P], F32)
+        woven23 = sbuf("woven23", [P, 4 * P], F32, "val_rows3")
+        woven = [woven01[:, : 2 * P], woven01[:, 2 * P :], woven23[:, : 2 * P], woven23[:, 2 * P :]]
+        turn_values(0, 6, nc.vector.tensor_copy)
+        turn_values(1, 2, nc.scalar.copy)
+        v01 = quantise("v01", woven01[:].bitcast(BF16), "val_rows1")
+        turn_values(2, 3, nc.scalar.copy)
+        turn_values(3, 1, nc.scalar.copy)
         v23 = quantise("v23", woven23[:].bitcast(BF16))
 
-        for first, (codes, scales), copy in ((0, v01, nc.scalar.copy), (2, v23, nc.vector.tensor_copy)):
-            result_ps = bank(6 + first // 2, [P, 2 * P])
+        for first, (codes, scales), number, copy in ((0, v01, 1, nc.scalar.copy), (2, v23, 7, nc.vector.tensor_copy)):
+            result_ps = bank(number, [P, 2 * P])
             product(result_ps[:], w_codes[:], w_scales[:], codes[:], scales[:])
             result = sbuf("result%d" % first, [P, 2 * P], F32)
             copy(result[:], result_ps[:])

@@ -42,15 +42,15 @@ def tile_attend_groupvotes_runcap_read_kernel(tc, query, keys_words, keys_scales
             nc.vector.quantize_mx(out=codes[:].bitcast(FP8X4), scales=scales[:], in_=woven)
             return codes, scales
 
-        def product(dst, lhs_codes, lhs_scales, rhs_codes, rhs_scales):
+        def product(dst, lhs_codes, lhs_scales, rhs_codes, rhs_scales, start=True, stop=True):
             nc.tensor.matmul_mx(
                 out=dst,
                 lhsT=lhs_codes.bitcast(FP8X4),
                 lhsT_scale=lhs_scales,
                 rhs=rhs_codes.bitcast(FP8X4),
                 rhs_scale=rhs_scales,
-                start=True,
-                stop=True,
+                start=start,
+                stop=stop,
             )
 
         key_bytes = sbuf("key_bytes", [P, T], U8)
@@ -93,48 +93,64 @@ def tile_attend_groupvotes_runcap_read_kernel(tc, query, keys_words, keys_scales
         q_woven = sbuf("q_woven", [P, Q, PACK], BF16)
         nc.scalar.copy(out=q_woven[:], in_=q_raw[:].rearrange("p j q -> p q j"))
         q_codes, q_scales = quantise("q", q_woven[:].rearrange("p q j -> p (q j)"))
+        neg_q_woven = sbuf("neg_q_woven", [P, Q, PACK], BF16)
+        nc.scalar.activation(out=neg_q_woven[:], in_=q_raw[:].rearrange("p j q -> p q j"), func=ACT.Copy, scale=-1.0)
+        neg_q_codes, neg_q_scales = quantise("neg_q", neg_q_woven[:].rearrange("p q j -> p (q j)"))
 
-        picked_words = {}
-        for h in range(2):
+        words_of = {}
+        for first, count in ((2, 1), (0, 2), (3, 1)):
             for side, offsets in enumerate((list_a, list_b)):
-                picked_words[side, h] = sbuf("picked_words%d%d" % (side, h), [P, HALF], U32)
-                nc.vector.tensor_copy(picked_words[side, h][:], key_words[:].indirect(offsets[:, 16 * h : 16 * (h + 1)]))
+                words = sbuf("picked_words%d%d" % (side, first), [P, count * P], U32)
+                nc.vector.tensor_copy(words[:], key_words[:].indirect(offsets[:, 8 * first : 8 * (first + count)]))
+                for c in range(count):
+                    words_of[side, first + c] = words[:, P * c : P * (c + 1)]
 
         lam_ps = bank(6, [P, Q])
         nc.tensor.transpose(lam_ps[:], lam_col[:].to_broadcast([P, P]), ident[:])
         lam_row = sbuf("lam_row", [P, Q], F32)
         nc.scalar.activation(out=lam_row[:], in_=lam_ps[:], func=ACT.Copy, scale=1.0 / GROUP)
 
-        def scores(side, h):
-            tile = bank(2 * side + h, [P, 2, Q])
-            for c in range(2):
-                slot = HALF * h + P * c
-                product(
-                    tile[:, c, :],
-                    picked_words[side, h][:, P * c : P * (c + 1)],
-                    picked_bytes[side][:, slot : slot + P],
-                    q_codes[:],
-                    q_scales[:],
-                )
-            return tile
+        def score(dst, side, chunk, negated=False, start=True, stop=True):
+            codes, scales = (neg_q_codes, neg_q_scales) if negated else (q_codes, q_scales)
+            product(dst, words_of[side, chunk], picked_bytes[side][:, P * chunk : P * (chunk + 1)], codes[:], scales[:], start, stop)
 
-        a_sb, b_ps, s_ps = [], [], []
-        for h in range(2):
-            a_ps = scores(0, h)
-            a_sb.append(sbuf("a_sb%d" % h, [P, 2, Q], F32))
-            nc.scalar.copy(out=a_sb[h][:], in_=a_ps[:])
-            b_ps.append(scores(1, h))
+        a_sb = [sbuf("a_sb%d" % h, [P, 2, Q], F32) for h in range(2)]
+        votes = [sbuf("vote%d" % h, [P, 2, Q], F32) for h in range(2)]
+
+        a2_ps = bank(1, [P, Q])
+        score(a2_ps[:], 0, 2)
+        nc.scalar.copy(out=a_sb[1][:, 0, :], in_=a2_ps[:])
+        b2_ps = bank(2, [P, Q])
+        score(b2_ps[:], 1, 2)
+        diff2 = sbuf("diff2", [P, Q], F32)
+        nc.vector.tensor_tensor(diff2[:], a_sb[1][:, 0, :], b2_ps[:], ALU.subtract)
+
+        diff01_ps = bank(3, [P, 2, Q])
+        for c in range(2):
+            score(diff01_ps[:, c, :], 0, c, start=(c == 0), stop=False)
+        a01_ps = bank(0, [P, 2, Q])
+        for c in range(2):
+            score(a01_ps[:, c, :], 0, c)
+        nc.scalar.copy(out=a_sb[0][:], in_=a01_ps[:])
+        for c in range(2):
+            score(diff01_ps[:, c, :], 1, c, negated=True, start=False, stop=(c == 1))
+        nc.scalar.activation(out=votes[0][:], in_=diff01_ps[:], func=ACT.Tanh)
+        nc.scalar.activation(out=votes[1][:, 0, :], in_=diff2[:], func=ACT.Tanh)
+
+        diff3_ps = bank(7, [P, Q])
+        score(diff3_ps[:], 0, 3, stop=False)
+        a3_ps = bank(1, [P, Q])
+        score(a3_ps[:], 0, 3)
+        score(diff3_ps[:], 1, 3, negated=True, start=False)
+        nc.scalar.activation(out=votes[1][:, 1, :], in_=diff3_ps[:], func=ACT.Tanh)
+        nc.scalar.copy(out=a_sb[1][:, 1, :], in_=a3_ps[:])
+
+        s_ps, sums = [], []
         for h in range(2):
             s_ps.append(bank(4 + h, [P, HALF]))
             for c in range(2):
                 nc.tensor.matmul(s_ps[h][:, P * c : P * (c + 1)], lhsT=a_sb[h][:, c, :], rhs=ident[:], is_transpose=True, start=(c == 0), stop=False)
 
-        votes, sums = [], []
-        for h in range(2):
-            diff = sbuf("diff%d" % h, [P, 2, Q], F32)
-            nc.vector.tensor_tensor(diff[:], a_sb[h][:], b_ps[h][:], ALU.subtract)
-            votes.append(sbuf("vote%d" % h, [P, 2, Q], F32))
-            nc.scalar.activation(out=votes[h][:], in_=diff[:], func=ACT.Tanh)
         for h in range(2):
             sums.append(sbuf("vote_sum%d" % h, [P, 2, Q // GROUP], F32))
             nc.vector.tensor_reduce(out=sums[h][:], in_=votes[h][:].rearrange("p c (v m) -> p c v m", m=GROUP), axis=AXIS.X, op=ALU.add)
@@ -154,13 +170,14 @@ def tile_attend_groupvotes_runcap_read_kernel(tc, query, keys_words, keys_scales
             nc.scalar.activation(out=picked[:], in_=val_rows[j][:].indirect(list_a[:]), func=ACT.Copy)
             return picked
 
-        neg_s, neg_max = [], []
+        neg_s = sbuf("neg_s", [P, 2, P, 2], F32)
+        halves = [slice(P // 2 * h, P // 2 * (h + 1)) for h in range(2)]
+        neg_max = []
         for h in range(2):
-            neg_s.append(sbuf("neg_s%d" % h, [P, HALF], F32))
             neg_max.append(sbuf("neg_max%d" % h, [P, 1], F32))
             nc.vector.tensor_scalar(
-                out=neg_s[h][:],
-                in0=s_ps[h][:],
+                out=neg_s[:, :, halves[h], :],
+                in0=s_ps[h][:].rearrange("q (s u j) -> q u s j", u=2, j=2),
                 scalar1=-1.0,
                 scalar2=(None if h == 0 else neg_max[0][:]),
                 op0=ALU.mult,
@@ -168,16 +185,27 @@ def tile_attend_groupvotes_runcap_read_kernel(tc, query, keys_words, keys_scales
                 accum_out=neg_max[h][:],
             )
         half_runs = HALF // RUN
-        run_sums, run_inv, factor = [], [], []
+        run_sums, run_inv = [], []
         row_sums = sbuf("row_sums", [P, 2], F32)
         picked = [pick_values(0), pick_values(1)]
-        p_tile = sbuf("p", [P, I], F32, "val_rows1")
-        p = [p_tile[:, :HALF], p_tile[:, HALF:]]
+        p = sbuf("p", [P, 2, P, 2], F32, "val_rows1")
         for h in range(2):
-            nc.scalar.activation(out=p[h], in_=neg_s[h][:], func=ACT.Exp, bias=neg_max[1][:], scale=-1.0, accum_out=row_sums[:, h : h + 1])
+            nc.scalar.activation(
+                out=p[:, :, halves[h], :],
+                in_=neg_s[:, :, halves[h], :],
+                func=ACT.Exp,
+                bias=neg_max[1][:],
+                scale=-1.0,
+                accum_out=row_sums[:, h : h + 1],
+            )
         for h in range(2):
             run_sums.append(sbuf("run_sums%d" % h, [P, half_runs], F32))
-            nc.vector.tensor_reduce(out=run_sums[h][:], in_=p[h].rearrange("q (g j) -> q g j", j=RUN), axis=AXIS.X, op=ALU.add)
+            nc.vector.tensor_reduce(
+                out=run_sums[h][:],
+                in_=p[:, :, halves[h], :].rearrange("q u (g e) j -> q g u (e j)", e=2),
+                axis=AXIS.XY,
+                op=ALU.add,
+            )
         row_sum = sbuf("row_sum", [P, 1], F32)
         nc.vector.tensor_tensor(row_sum[:], row_sums[:, 0:1], row_sums[:, 1:2], ALU.add)
         row_inv = sbuf("row_inv", [P, 1], F32)
@@ -186,34 +214,30 @@ def tile_attend_groupvotes_runcap_read_kernel(tc, query, keys_words, keys_scales
             nc.vector.reciprocal(run_inv[h][:], run_sums[h][:])
             if h == 0:
                 nc.vector.reciprocal(row_inv[:], row_sum[:])
+        factor = sbuf("factor", [P, P], F32)
         for h in range(2):
-            factor.append(sbuf("factor%d" % h, [P, half_runs, 2], F32))
             nc.vector.tensor_scalar(
-                out=factor[h][:],
+                out=factor[:, halves[h]].rearrange("q (g e) -> q g e", e=2),
                 in0=run_inv[h][:].unsqueeze(2).to_broadcast([P, half_runs, 2]),
                 scalar1=cap_col[:],
                 scalar2=row_inv[:],
                 op0=ALU.mult,
                 op1=ALU.min,
             )
-        w_dealt = sbuf("w_dealt", [P, PACK, P], F32)
-        for h in range(2):
-            nc.vector.tensor_tensor(
-                w_dealt[:, :, P // 2 * h : P // 2 * (h + 1)].rearrange("q r (b s) -> q b r s", s=4),
-                p[h].rearrange("q (b s r) -> q b r s", s=4, r=PACK),
-                factor[h][:].rearrange("q (b g) e -> q b (g e)", g=2).unsqueeze(2).to_broadcast([P, P // 8, PACK, 4]),
-                ALU.mult,
-            )
-        wt_ps = bank(0, [P, PACK, Q])
+        pt_ps = bank(0, [P, PACK, Q])
         for r in range(PACK):
-            nc.tensor.transpose(wt_ps[:, r, :], w_dealt[:, r, :], ident[:])
-        w_woven = sbuf("w_woven", [P, Q, PACK], BF16)
+            nc.tensor.transpose(pt_ps[:, r, :], p[:, r // 2, :, r % 2], ident[:])
+        factor_ps = bank(4, [P, Q])
+        nc.tensor.transpose(factor_ps[:], factor[:], ident[:])
+        pt_os = sbuf("pt_os", [P, Q, PACK], F32, "run_inv0")
         nc.vector.tensor_tensor(
-            w_woven[:],
-            wt_ps[:].rearrange("s r q -> s q r"),
+            pt_os[:],
+            pt_ps[:].rearrange("s r q -> s q r"),
             os_cols[:].unsqueeze(1).to_broadcast([P, Q, PACK]),
             ALU.mult,
         )
+        w_woven = sbuf("w_woven", [P, Q, PACK], BF16)
+        nc.vector.tensor_tensor(w_woven[:], pt_os[:], factor_ps[:].unsqueeze(2).to_broadcast([P, Q, PACK]), ALU.mult)
         w_codes, w_scales = quantise("w", w_woven[:].rearrange("s q r -> s (q r)"))
 
         def turn_values(j, number, copy):
@@ -221,22 +245,27 @@ def tile_attend_groupvotes_runcap_read_kernel(tc, query, keys_words, keys_scales
             turned = bank(number, [P, 2, P])
             for u in range(2):
                 nc.tensor.transpose(turned[:, u, :], pairs[:, u::2], ident[:])
-            copy(woven[j].rearrange("s (e u) -> s e u", u=2), turned[:].rearrange("s u e -> s e u"))
+            copy(woven[j][:].rearrange("s (e u) -> s e u", u=2), turned[:].rearrange("s u e -> s e u"))
+            cols = slice(P * j, P * (j + 1))
+            nc.vector.quantize_mx(out=v_codes[:, cols].bitcast(FP8X4), scales=v_scales[:, cols], in_=woven[j][:].bitcast(BF16))
 
         picked.extend([pick_values(2), pick_values(3)])
-        woven01 = sbuf("woven01", [P, 4 * P], F32)
-        woven23 = sbuf("woven23", [P, 4 * P], F32, "val_rows3")
-        woven = [woven01[:, : 2 * P], woven01[:, 2 * P :], woven23[:, : 2 * P], woven23[:, 2 * P :]]
+        woven = [sbuf("woven%d" % j, [P, 2 * P], F32, "val_rows3" if j == 2 else None) for j in range(E // P)]
+        v_codes = sbuf("v_codes", [P, E], U32)
+        v_scales = sbuf("v_scales", [P, E], U8)
         turn_values(0, 6, nc.vector.tensor_copy)
         turn_values(1, 2, nc.scalar.copy)
-        v01 = quantise("v01", woven01[:].bitcast(BF16), "val_rows1")
         turn_values(2, 3, nc.scalar.copy)
         turn_values(3, 1, nc.scalar.copy)
-        v23 = quantise("v23", woven23[:].bitcast(BF16))
 
-        for first, (codes, scales), number, copy in ((0, v01, 1, nc.scalar.copy), (2, v23, 7, nc.vector.tensor_copy)):
-            result_ps = bank(number, [P, 2 * P])
-            product(result_ps[:], w_codes[:], w_scales[:], codes[:], scales[:])
-            result = sbuf("result%d" % first, [P, 2 * P], F32)
-            copy(result[:], result_ps[:])
-            nc.sync.dma_start(out=out[:, first * P : (first + 2) * P], in_=result[:])
+        early_ps = bank(3, [P, 3 * P])
+        for cols in (slice(0, 2 * P), slice(2 * P, 3 * P)):
+            product(early_ps[:, cols], w_codes[:], w_scales[:], v_codes[:, cols], v_scales[:, cols])
+        early = sbuf("early", [P, 3 * P], F32)
+        nc.scalar.copy(early[:], early_ps[:])
+        nc.sync.dma_start(out=out[:, : 3 * P], in_=early[:])
+        last_ps = bank(7, [P, P])
+        product(last_ps[:], w_codes[:], w_scales[:], v_codes[:, 3 * P :], v_scales[:, 3 * P :])
+        last = sbuf("last", [P, P], F32)
+        nc.vector.tensor_copy(last[:], last_ps[:])
+        nc.sync.dma_start(out=out[:, 3 * P :], in_=last[:])

from contextlib import ExitStack

import concourse.mybir as mybir
from concourse.masks import make_identity

D, T, I, Q, E = 512, 2048, 512, 128, 512
P = 128
PACK = 4
GROUP = 8
RUN = 8
HALF = I // 2
FLOPS = 2 * D * I * Q * 2 + 2 * I * Q * E

F32 = mybir.dt.float32
BF16 = mybir.dt.bfloat16
I32 = mybir.dt.int32
U32 = mybir.dt.uint32
U16 = mybir.dt.uint16
U8 = mybir.dt.uint8
FP8X4 = mybir.dt.float8_e4m3fn_x4
ALU = mybir.AluOpType
ACT = mybir.ActivationFunctionType
AXIS = mybir.AxisListType


def tile_attend_groupvotes_runcap_read_kernel(tc, query, keys_words, keys_scales, lam, cap, slot_factor, vals, offs, offs2, out):
    nc = tc.nc
    with ExitStack() as ctx:
        sb = ctx.enter_context(tc.tile_pool(name="sb", bufs=1))
        ps = ctx.enter_context(tc.psum_pool(name="ps", bufs=1))

        def sbuf(name, shape, dtype, reuse=None):
            return sb.tile(shape, dtype, name=name, tag=reuse or name, align_bytes=64)

        def bank(number, shape):
            return ps.tile(shape, F32, name="bank%d" % number, tag="bank%d" % number)

        def quantise(name, woven, reuse=None):
            width = woven.shape[1] // PACK
            codes = sbuf(name + "_codes", [P, width], U32, reuse)
            scales = sbuf(name + "_scales", [P, width], U8)
            nc.vector.quantize_mx(out=codes[:].bitcast(FP8X4), scales=scales[:], in_=woven)
            return codes, scales

        def product(dst, lhs_codes, lhs_scales, rhs_codes, rhs_scales, start=True, stop=True):
            nc.tensor.matmul_mx(
                out=dst,
                lhsT=lhs_codes.bitcast(FP8X4),
                lhsT_scale=lhs_scales,
                rhs=rhs_codes.bitcast(FP8X4),
                rhs_scale=rhs_scales,
                start=start,
                stop=stop,
            )

        key_bytes = sbuf("key_bytes", [P, T], U8)
        nc.gpsimd.memset(key_bytes[:].bitcast(I32), 0)
        list_a = sb.tile([P, I // 16], U16)
        nc.sync.dma_start(list_a[:], offs)
        scale_rows = keys_scales[0].bitcast(I32)
        for quad in range(4):
            nc.sync.dma_start(out=key_bytes[32 * quad : 32 * quad + 4, :].bitcast(I32), in_=scale_rows[4 * quad : 4 * quad + 4, :])
        list_b = sb.tile([P, I // 16], U16)
        nc.sync.dma_start(list_b[:], offs2)
        q_raw = sbuf("q_raw", [P, PACK, Q], F32)
        nc.sync.dma_start(out=q_raw[:], in_=query.rearrange("(p j) q -> p j q", j=PACK))
        key_words = sbuf("key_words", [P, T], U32)
        nc.sync.dma_start(out=key_words[:].bitcast(I32), in_=keys_words[0].rearrange("p t r -> p (t r)").bitcast(I32))
        lam_col = sbuf("lam_col", [P, 1], F32)
        nc.sync.dma_start(out=lam_col[:], in_=lam.rearrange("o q -> q o"))

        def load_values(j):
            rows = sbuf("val_rows%d" % j, [P, T], F32)
            nc.sync.dma_start(out=rows[:], in_=vals[P * j : P * (j + 1), :])
            return rows

        val_rows = [load_values(0)]
        cap_col = sbuf("cap_col", [P, 1], F32)
        nc.sync.dma_start(out=cap_col[:], in_=cap)
        os_cols = sbuf("os_cols", [P, PACK], F32)
        nc.sync.dma_start(out=os_cols[:], in_=slot_factor.rearrange("o (p r) -> p (o r)", r=PACK))
        for j in range(1, E // P):
            val_rows.append(load_values(j))

        ident = sbuf("ident", [P, P], F32)
        make_identity(nc, ident[:])

        picked_bytes = []
        for side, offsets in enumerate((list_a, list_b)):
            picked_bytes.append(sbuf("picked_bytes%d" % side, [P, I], U8))
            nc.vector.tensor_copy(picked_bytes[side][:], key_bytes[:].indirect(offsets[:]))

        q_woven = sbuf("q_woven", [P, Q, PACK], BF16)
        nc.scalar.copy(out=q_woven[:], in_=q_raw[:].rearrange("p j q -> p q j"))
        q_codes, q_scales = quantise("q", q_woven[:].rearrange("p q j -> p (q j)"))
        neg_q_woven = sbuf("neg_q_woven", [P, Q, PACK], BF16)
        nc.scalar.activation(out=neg_q_woven[:], in_=q_raw[:].rearrange("p j q -> p q j"), func=ACT.Copy, scale=-1.0)
        neg_q_codes, neg_q_scales = quantise("neg_q", neg_q_woven[:].rearrange("p q j -> p (q j)"))

        words_of = {}
        for first, count in ((2, 1), (0, 2), (3, 1)):
            for side, offsets in enumerate((list_a, list_b)):
                words = sbuf("picked_words%d%d" % (side, first), [P, count * P], U32)
                nc.vector.tensor_copy(words[:], key_words[:].indirect(offsets[:, 8 * first : 8 * (first + count)]))
                for c in range(count):
                    words_of[side, first + c] = words[:, P * c : P * (c + 1)]

        lam_ps = bank(6, [P, Q])
        nc.tensor.transpose(lam_ps[:], lam_col[:].to_broadcast([P, P]), ident[:])
        lam_row = sbuf("lam_row", [P, Q], F32)
        nc.scalar.activation(out=lam_row[:], in_=lam_ps[:], func=ACT.Copy, scale=1.0 / GROUP)

        def score(dst, side, chunk, negated=False, start=True, stop=True):
            codes, scales = (neg_q_codes, neg_q_scales) if negated else (q_codes, q_scales)
            product(dst, words_of[side, chunk], picked_bytes[side][:, P * chunk : P * (chunk + 1)], codes[:], scales[:], start, stop)

        a_sb = [sbuf("a_sb%d" % h, [P, 2, Q], F32) for h in range(2)]
        votes = [sbuf("vote%d" % h, [P, 2, Q], F32) for h in range(2)]

        a2_ps = bank(1, [P, Q])
        score(a2_ps[:], 0, 2)
        nc.scalar.copy(out=a_sb[1][:, 0, :], in_=a2_ps[:])
        b2_ps = bank(2, [P, Q])
        score(b2_ps[:], 1, 2)
        diff2 = sbuf("diff2", [P, Q], F32)
        nc.vector.tensor_tensor(diff2[:], a_sb[1][:, 0, :], b2_ps[:], ALU.subtract)

        diff01_ps = bank(3, [P, 2, Q])
        for c in range(2):
            score(diff01_ps[:, c, :], 0, c, start=(c == 0), stop=False)
        a01_ps = bank(0, [P, 2, Q])
        for c in range(2):
            score(a01_ps[:, c, :], 0, c)
        nc.scalar.copy(out=a_sb[0][:], in_=a01_ps[:])
        for c in range(2):
            score(diff01_ps[:, c, :], 1, c, negated=True, start=False, stop=(c == 1))
        nc.scalar.activation(out=votes[0][:], in_=diff01_ps[:], func=ACT.Tanh)
        nc.scalar.activation(out=votes[1][:, 0, :], in_=diff2[:], func=ACT.Tanh)

        diff3_ps = bank(7, [P, Q])
        score(diff3_ps[:], 0, 3, stop=False)
        a3_ps = bank(1, [P, Q])
        score(a3_ps[:], 0, 3)
        score(diff3_ps[:], 1, 3, negated=True, start=False)
        nc.scalar.activation(out=votes[1][:, 1, :], in_=diff3_ps[:], func=ACT.Tanh)
        nc.scalar.copy(out=a_sb[1][:, 1, :], in_=a3_ps[:])

        s_ps, sums = [], []
        for h in range(2):
            s_ps.append(bank(4 + h, [P, HALF]))
            for c in range(2):
                nc.tensor.matmul(s_ps[h][:, P * c : P * (c + 1)], lhsT=a_sb[h][:, c, :], rhs=ident[:], is_transpose=True, start=(c == 0), stop=False)

        for h in range(2):
            sums.append(sbuf("vote_sum%d" % h, [P, 2, Q // GROUP], F32))
            nc.vector.tensor_reduce(out=sums[h][:], in_=votes[h][:].rearrange("p c (v m) -> p c v m", m=GROUP), axis=AXIS.X, op=ALU.add)
        for h in range(2):
            lift = sbuf("lift%d" % h, [P, 2, Q], F32)
            nc.vector.tensor_tensor(
                lift[:].rearrange("p c (v m) -> p c v m", m=GROUP),
                sums[h][:].unsqueeze(3).to_broadcast([P, 2, Q // GROUP, GROUP]),
                lam_row[:].rearrange("p (v m) -> p v m", m=GROUP).unsqueeze(1).to_broadcast([P, 2, Q // GROUP, GROUP]),
                ALU.mult,
            )
            for c in range(2):
                nc.tensor.matmul(s_ps[h][:, P * c : P * (c + 1)], lhsT=lift[:, c, :], rhs=ident[:], is_transpose=True, start=False, stop=(c == 1))

        def pick_values(j):
            picked = sbuf("picked%d" % j, [P, I], BF16)
            nc.scalar.activation(out=picked[:], in_=val_rows[j][:].indirect(list_a[:]), func=ACT.Copy)
            return picked

        neg_s = sbuf("neg_s", [P, 2, P, 2], F32)
        halves = [slice(P // 2 * h, P // 2 * (h + 1)) for h in range(2)]
        neg_max = []
        for h in range(2):
            neg_max.append(sbuf("neg_max%d" % h, [P, 1], F32))
            nc.vector.tensor_scalar(
                out=neg_s[:, :, halves[h], :],
                in0=s_ps[h][:].rearrange("q (s u j) -> q u s j", u=2, j=2),
                scalar1=-1.0,
                scalar2=(None if h == 0 else neg_max[0][:]),
                op0=ALU.mult,
                op1=ALU.min,
                accum_out=neg_max[h][:],
            )
        half_runs = HALF // RUN
        run_sums, run_inv = [], []
        row_sums = sbuf("row_sums", [P, 2], F32)
        picked = [pick_values(0), pick_values(1)]
        p = sbuf("p", [P, 2, P, 2], F32, "val_rows1")
        for h in range(2):
            nc.scalar.activation(
                out=p[:, :, halves[h], :],
                in_=neg_s[:, :, halves[h], :],
                func=ACT.Exp,
                bias=neg_max[1][:],
                scale=-1.0,
                accum_out=row_sums[:, h : h + 1],
            )
        for h in range(2):
            run_sums.append(sbuf("run_sums%d" % h, [P, half_runs], F32))
            nc.vector.tensor_reduce(
                out=run_sums[h][:],
                in_=p[:, :, halves[h], :].rearrange("q u (g e) j -> q g u (e j)", e=2),
                axis=AXIS.XY,
                op=ALU.add,
            )
        row_sum = sbuf("row_sum", [P, 1], F32)
        nc.vector.tensor_tensor(row_sum[:], row_sums[:, 0:1], row_sums[:, 1:2], ALU.add)
        row_inv = sbuf("row_inv", [P, 1], F32)
        for h in range(2):
            run_inv.append(sbuf("run_inv%d" % h, [P, half_runs], F32))
            nc.vector.reciprocal(run_inv[h][:], run_sums[h][:])
            if h == 0:
                nc.vector.reciprocal(row_inv[:], row_sum[:])
        factor = sbuf("factor", [P, P], F32)
        for h in range(2):
            nc.vector.tensor_scalar(
                out=factor[:, halves[h]].rearrange("q (g e) -> q g e", e=2),
                in0=run_inv[h][:].unsqueeze(2).to_broadcast([P, half_runs, 2]),
                scalar1=cap_col[:],
                scalar2=row_inv[:],
                op0=ALU.mult,
                op1=ALU.min,
            )
        pt_ps = bank(0, [P, PACK, Q])
        for r in range(PACK):
            nc.tensor.transpose(pt_ps[:, r, :], p[:, r // 2, :, r % 2], ident[:])
        factor_ps = bank(4, [P, Q])
        nc.tensor.transpose(factor_ps[:], factor[:], ident[:])
        pt_os = sbuf("pt_os", [P, Q, PACK], F32, "run_inv0")
        nc.vector.tensor_tensor(
            pt_os[:],
            pt_ps[:].rearrange("s r q -> s q r"),
            os_cols[:].unsqueeze(1).to_broadcast([P, Q, PACK]),
            ALU.mult,
        )
        w_woven = sbuf("w_woven", [P, Q, PACK], BF16)
        nc.vector.tensor_tensor(w_woven[:], pt_os[:], factor_ps[:].unsqueeze(2).to_broadcast([P, Q, PACK]), ALU.mult)
        w_codes, w_scales = quantise("w", w_woven[:].rearrange("s q r -> s (q r)"))

        def turn_values(j, number, copy):
            pairs = picked[j][:].bitcast(F32)
            turned = bank(number, [P, 2, P])
            for u in range(2):
                nc.tensor.transpose(turned[:, u, :], pairs[:, u::2], ident[:])
            copy(woven[j][:].rearrange("s (e u) -> s e u", u=2), turned[:].rearrange("s u e -> s e u"))
            cols = slice(P * j, P * (j + 1))
            nc.vector.quantize_mx(out=v_codes[:, cols].bitcast(FP8X4), scales=v_scales[:, cols], in_=woven[j][:].bitcast(BF16))

        picked.extend([pick_values(2), pick_values(3)])
        woven = [sbuf("woven%d" % j, [P, 2 * P], F32, "val_rows3" if j == 2 else None) for j in range(E // P)]
        v_codes = sbuf("v_codes", [P, E], U32)
        v_scales = sbuf("v_scales", [P, E], U8)
        turn_values(0, 6, nc.vector.tensor_copy)
        turn_values(1, 2, nc.scalar.copy)
        turn_values(2, 3, nc.scalar.copy)
        turn_values(3, 1, nc.scalar.copy)

        early_ps = bank(3, [P, 3 * P])
        for cols in (slice(0, 2 * P), slice(2 * P, 3 * P)):
            product(early_ps[:, cols], w_codes[:], w_scales[:], v_codes[:, cols], v_scales[:, cols])
        early = sbuf("early", [P, 3 * P], F32)
        nc.scalar.copy(early[:], early_ps[:])
        nc.sync.dma_start(out=out[:, : 3 * P], in_=early[:])
        last_ps = bank(7, [P, P])
        product(last_ps[:], w_codes[:], w_scales[:], v_codes[:, 3 * P :], v_scales[:, 3 * P :])
        last = sbuf("last", [P, P], F32)
        nc.vector.tensor_copy(last[:], last_ps[:])
        nc.sync.dma_start(out=out[:, 3 * P :], in_=last[:])
